import numpy as np
import ml_dtypes


def mxq(x, axis, fmt="e4m3"):
    dtype, down = {"e4m3": (ml_dtypes.float8_e4m3fn, 7), "e5m2": (ml_dtypes.float8_e5m2, 14)}[fmt]
    v = np.moveaxis(np.asarray(x, np.float32).astype(ml_dtypes.bfloat16).astype(np.float64), axis, -1)
    blocks = v.reshape(v.shape[:-1] + (-1, 32))
    amax = np.abs(blocks).max(-1, keepdims=True)
    byte = np.maximum(np.where(amax > 0, np.frexp(amax)[1] - 1 + 127, 0) - down, 1)
    scale = np.exp2(byte - 127.0)
    codes = (blocks / scale).astype(np.float32).astype(dtype).astype(np.float64)
    return np.moveaxis((codes * scale).reshape(v.shape), -1, axis)


WIDE = False


def mx_kscale(k):
    if not WIDE:
        return np.ones(k)
    levels = np.array([30, -30])
    if k % 512:
        return np.exp2(np.random.permutation(np.resize(levels, k // 32))).repeat(32)
    a = np.empty((k // 512, 16))
    for p in range(k // 512):
        a[p, :8] = np.random.permutation(np.resize(levels, 8))
        for g in range(8):
            far = levels[np.abs(levels - a[p, g]) >= 10]
            a[p, g + 8] = far[np.random.randint(len(far))]
    return np.exp2(a.ravel()).repeat(32)


def f64(x):
    return np.asarray(x).astype(np.float64)


def striped(idx):
    return np.tile(np.asarray(idx).reshape(-1, 16).T, (8, 1)).astype(np.uint16)


def unstriped(offs):
    return offs[:16].T.reshape(-1).astype(np.int64)


E2M1 = np.array([0.0, 0.5, 1.0, 1.5, 2.0, 3.0, 4.0, 6.0, -0.0, -0.5, -1.0, -1.5, -2.0, -3.0, -4.0, -6.0])


def pack_weight(w, fmt):
    k, n = w.shape
    w = f64(np.asarray(w, np.float32).astype(ml_dtypes.bfloat16)).reshape(k // 32, 32, n)
    amax = np.abs(w).max(1)
    if fmt in ("e4m3", "e5m2"):
        byte = np.frexp(amax)[1] - 1 + 127 - (7 if fmt == "e4m3" else 14)
    else:
        mant, ex = np.frexp(amax / 6.0)
        byte = np.where(mant > 0.5, ex, ex - 1) + 127
    byte = np.clip(np.where(amax > 0, byte, 1), 1, 254)
    scaled = (w * np.exp2(127.0 - byte)[:, None, :]).reshape(k, n).astype(np.float32)
    by_word = np.ascontiguousarray(scaled.reshape(k // 512, 128, 4, n).transpose(0, 1, 3, 2))
    if fmt in ("e4m3", "e5m2"):
        words = by_word.astype(ml_dtypes.float8_e4m3fn if fmt == "e4m3" else ml_dtypes.float8_e5m2).view(np.uint8)
    else:
        c = by_word.astype(ml_dtypes.float4_e2m1fn).view(np.uint8) & 0xF
        words = (c[..., 0::2] | (c[..., 1::2] << 4)).reshape(k // 512, 128, 2 * n)
    return np.ascontiguousarray(words), np.ascontiguousarray(byte.astype(np.uint8).reshape(k // 512, 16, n))


def unpack_weight(words, scales, fmt):
    g, _, n = scales.shape
    words = np.ascontiguousarray(words).reshape(g, 128, n, -1)
    if fmt in ("e4m3", "e5m2"):
        vals = words.view(ml_dtypes.float8_e4m3fn if fmt == "e4m3" else ml_dtypes.float8_e5m2).astype(np.float64)
    else:
        nib = np.empty((g, 128, n, 4), np.uint8)
        nib[..., 0::2] = words & 0xF
        nib[..., 1::2] = words >> 4
        vals = E2M1[nib]
    vals = vals * np.repeat(np.exp2(scales.astype(np.float64) - 127.0), 8, axis=1)[..., None]
    return vals.transpose(0, 1, 3, 2).reshape(g * 512, n)


def sigmoid(v):
    return 1.0 / (1.0 + np.exp(-v))


def sgn(shape):
    return np.random.uniform(0.5, 2.0, shape) * np.where(np.random.standard_normal(shape) < 0, -1.0, 1.0)


K, T, J, R, F, Z, O, N, S, E = 512, 1024, 256, 512, 512, 1024, 128, 256, 1024, 1024


def setup_inputs():
    n = np.random.standard_normal
    idx = np.random.permutation(T)[:J]
    idx2 = np.random.permutation(Z)[:J]
    idx3 = np.random.permutation(J)[:O]
    idx4 = np.random.permutation(J)[:O]
    idx5 = np.random.permutation(J)[:O]
    idx6 = np.random.permutation(S)[:N]
    idx7 = np.random.permutation(E)[:O]
    ff = mx_kscale(F)
    fk = mx_kscale(K)
    fr = mx_kscale(R)
    xop = pack_weight(n((F, Z)) / ff[:, None], "e2m1")
    wp = pack_weight(n((K, R)) * 1 / np.sqrt(K) / fk[:, None], "e2m1")
    w2p = pack_weight(n((F, R)) * 1 / np.sqrt(F) * ff[:, None], "e5m2")
    vsp = pack_weight(n((R, S)) * 1 / np.sqrt(R) / fr[:, None], "e5m2")
    return {
        "xo_words": xop[0],
        "xo_scales": xop[1],
        "cq": (np.random.randint(-7, 8, (K, T)).astype(np.float64)).astype(np.float32),
        "gs": (np.random.uniform(0.1, 0.4, (K, 1)) * fk[:, None]).astype(np.float32),
        "w_words": wp[0],
        "w_scales": wp[1],
        "w2_words": w2p[0],
        "w2_scales": w2p[1],
        "sa": (np.random.uniform(0.5, 1.6, (R, 1)) * fr[:, None]).astype(np.float32),
        "sb": (np.random.uniform(0.5, 1.6, (R, 1)) * fr[:, None]).astype(np.float32),
        "sg": (sgn((R, 1))).astype(np.float32),
        "vs_words": vsp[0],
        "vs_scales": vsp[1],
        "offs": striped(idx),
        "offs2": striped(idx2),
        "offs3": striped(idx3),
        "offs4": striped(idx4),
        "offs5": striped(idx5),
        "offs6": striped(idx6),
        "offs7": striped(idx7),
    }


def reference(xo_words, xo_scales, cq, gs, w_words, w_scales, w2_words, w2_scales, sa, sb, sg, vs_words, vs_scales, offs, offs2, offs3, offs4, offs5, offs6, offs7):
    idx = unstriped(offs)
    idx2 = unstriped(offs2)
    idx3 = unstriped(offs3)
    idx4 = unstriped(offs4)
    idx5 = unstriped(offs5)
    idx6 = unstriped(offs6)
    idx7 = unstriped(offs7)
    xou = unpack_weight(xo_words, xo_scales, "e2m1")
    wu = unpack_weight(w_words, w_scales, "e2m1")
    w2u = unpack_weight(w2_words, w2_scales, "e5m2")
    vsu = unpack_weight(vs_words, vs_scales, "e5m2")
    x1 = f64(cq)[:, idx] * f64(gs)
    x1q = mxq(x1, 0, "e4m3")
    a = wu.T @ x1q
    xoidx2g = xou[:, idx2]
    b = w2u.T @ xoidx2g
    lb = b[:, 0:1]
    hid = a[:, idx3] * f64(sa) * sigmoid(a[:, idx4] * f64(sg) + lb) - b[:, idx5] * f64(sb)
    vsidx6g = vsu[:, idx6]
    hidq = mxq(hid, 0, "e4m3")
    p = vsidx6g.T @ hidq
    y = np.zeros((N, E))
    y[:, idx7] = p
    return y

@@ -1,0 +1,207 @@
+from contextlib import ExitStack
+
+import concourse.mybir as mybir
+
+K, T, J, R, F, Z, O, N, S, E = 512, 1024, 256, 512, 512, 1024, 128, 256, 1024, 1024
+FLOPS = 2 * K * R * J + 2 * F * R * J + 2 * R * N * O
+
+P = 128
+PACK = 4
+F32 = mybir.dt.float32
+BF16 = mybir.dt.bfloat16
+I32 = mybir.dt.int32
+U32 = mybir.dt.uint32
+U16 = mybir.dt.uint16
+U8 = mybir.dt.uint8
+E4M3 = mybir.dt.float8_e4m3fn_x4
+E5M2 = mybir.dt.float8_e5m2_x4
+E2M1 = mybir.dt.float4_e2m1fn_x4
+ACT = mybir.ActivationFunctionType
+ALU = mybir.AluOpType
+
+
+def tile_list_offsetlead_codednote_store_scattered_kernel(
+    tc, xo_words, xo_scales, cq, gs, w_words, w_scales, w2_words, w2_scales, sa, sb, sg,
+    vs_words, vs_scales, offs, offs2, offs3, offs4, offs5, offs6, offs7, out,
+):
+    nc = tc.nc
+    with ExitStack() as ctx:
+        sb_pool = ctx.enter_context(tc.tile_pool(name="held", bufs=1))
+        table = ctx.enter_context(tc.tile_pool(name="table", bufs=1))
+        psum = ctx.enter_context(tc.psum_pool(name="psum", bufs=1))
+
+        def tile(name, shape, dtype, tag=None):
+            return sb_pool.tile(shape, dtype, name=name, tag=tag or name, align_bytes=64)
+
+        def load_list(name, src):
+            dst = sb_pool.tile(list(src.shape), U16, name=name)
+            nc.sync.dma_start(dst[:], src)
+            return dst
+
+        def load_column_vector(name, src):
+            dst = tile(name, [P, PACK], F32)
+            nc.gpsimd.dma_start(dst[:], src.rearrange("(p t) o -> p (t o)", t=PACK))
+            return dst
+
+        def load_scale_rows(stage, first, scales):
+            rows = scales[0].bitcast(I32).rearrange("(h q r) c -> q r h c", h=2, q=2)
+            for q in range(2):
+                part = first + 32 * q
+                nc.sync.dma_start(stage[part : part + 4].bitcast(I32), rows[q])
+
+        def spread_scale_rows(plane, stage, first):
+            for h in range(2):
+                nc.vector.tensor_copy(plane[64 * h : 64 * h + 64, :].bitcast(I32),
+                                      stage[first : first + 64, h, :].bitcast(I32))
+
+        xo_stage = tile("xo_stage", [P, 2, Z], U8)
+        w2_stage = tile("w2_stage", [P, 2, R], U8)
+        w_stage = tile("w_stage", [P, 2, R], U8)
+        vs_stage = tile("vs_stage", [P, 2, S], U8)
+        pages = [tile("page%d" % h, [P, E], F32) for h in range(2)]
+        nc.vector.memset(xo_stage[0:64].bitcast(I32), 0)
+        nc.gpsimd.memset(w2_stage[64:128].bitcast(I32), 0)
+        nc.vector.memset(w_stage[0:64].bitcast(I32), 0)
+        nc.vector.memset(vs_stage[64:128].bitcast(I32), 0)
+        for page in pages:
+            nc.vector.memset(page[:], 0.0)
+
+        gs_t = load_column_vector("gs_t", gs)
+        sb_t = load_column_vector("sb_t", sb)
+        sg_t = load_column_vector("sg_t", sg)
+        sa_t = load_column_vector("sa_t", sa)
+
+        xo_w = tile("xo_w", [P, Z], U16)
+        w2_raw = tile("w2_raw", [P, R], U32)
+        w_raw = tile("w_raw", [P, R], U16)
+        vs_w = tile("vs_w", [P, S], U32)
+        cq_t = [table.tile([P, T], F32, name="cq%d" % t, align_bytes=64, offset=4 * T * t) for t in range(PACK)]
+        cq_rows = cq.rearrange("(p t) c -> t p c", t=PACK)
+
+        nc.sync.dma_start(xo_w[:].bitcast(I32), xo_words[0].bitcast(I32))
+        load_scale_rows(xo_stage, 0, xo_scales)
+        l2 = load_list("l2", offs2)
+        nc.sync.dma_start(w2_raw[:].bitcast(I32), w2_words[0].rearrange("p c r -> p (c r)").bitcast(I32))
+        load_scale_rows(w2_stage, 64, w2_scales)
+        nc.sync.dma_start(cq_t[0][:], cq_rows[0])
+        l1 = load_list("l1", offs)
+        load_scale_rows(w_stage, 0, w_scales)
+        nc.sync.dma_start(cq_t[1][:], cq_rows[1])
+        nc.sync.dma_start(cq_t[2][:], cq_rows[2])
+        load_scale_rows(vs_stage, 64, vs_scales)
+        l6 = load_list("l6", offs6)
+        nc.sync.dma_start(cq_t[3][:], cq_rows[3])
+        nc.sync.dma_start(w_raw[:].bitcast(I32), w_words[0].bitcast(I32))
+        l5 = load_list("l5", offs5)
+        l4 = load_list("l4", offs4)
+        l3 = load_list("l3", offs3)
+        nc.sync.dma_start(vs_w[:].bitcast(I32), vs_words[0].rearrange("p c r -> p (c r)").bitcast(I32))
+        l7 = load_list("l7", offs7)
+
+        xo_plane = tile("xo_plane", [P, Z], U8)
+        xo_gw = tile("xo_gw", [P, J], U16)
+        xo_gs = tile("xo_gs", [P, J], U8)
+        nc.vector.tensor_copy(xo_gw[:], xo_w[:].indirect(l2[:]))
+        spread_scale_rows(xo_plane, xo_stage, 0)
+        nc.vector.tensor_copy(xo_gs[:], xo_plane[:].indirect(l2[:]))
+
+        w2_p = tile("w2_p", [P, PACK, P], U32)
+        nc.scalar.copy(w2_p[:].rearrange("p t m -> p m t"), w2_raw[:].rearrange("p (m t) -> p m t", t=PACK))
+        w2_plane = tile("w2_plane", [P, PACK, P], U8)
+        nc.vector.tensor_copy(w2_stage[0:64, 1, :].bitcast(I32), w2_stage[64:128, 0, :].bitcast(I32))
+        nc.vector.tensor_copy(w2_plane[:], w2_stage[:, 1, :].rearrange("p (m t) -> p t m", t=PACK))
+        w_plane = tile("w_plane", [P, PACK, P], U8)
+        nc.vector.tensor_copy(w_stage[64:128, 0, :].bitcast(I32), w_stage[0:64, 1, :].bitcast(I32))
+        nc.vector.tensor_copy(w_plane[:], w_stage[:, 0, :].rearrange("p (m t) -> p t m", t=PACK))
+
+        b_ps = [psum.tile([P, J], F32, name="b_ps%d" % t, tag="bank_b%d" % t) for t in range(PACK)]
+        b_t = [table.tile([P, J], F32, name="b%d" % t, align_bytes=64, offset=4 * T * (1 + t // 2) + 4 * J * (t % 2))
+               for t in range(PACK)]
+        for t in range(PACK):
+            nc.tensor.matmul_mx(b_ps[t][:], lhsT=w2_p[:, t, :].bitcast(E5M2), lhsT_scale=w2_plane[:, t, :],
+                                rhs=xo_gw[:].bitcast(E2M1), rhs_scale=xo_gs[:], start=True, stop=True)
+
+        x1_pair = [tile("x1_pair%d" % u, [P, 2, J], BF16) for u in range(2)]
+        x1_il = [tile("x1_il%d" % h, [P, P, PACK], BF16) for h in range(2)]
+
+        def gather_x1(t):
+            nc.scalar.activation(x1_pair[t // 2][:, t % 2, :], cq_t[t][:].indirect(l1[:]), ACT.Copy,
+                                 scale=gs_t[:, t : t + 1])
+
+        def interleave_x1(u):
+            for h in range(2):
+                nc.vector.tensor_copy(x1_il[h][:, :, 2 * u : 2 * u + 2],
+                                      x1_pair[u][:, :, h * P : (h + 1) * P].rearrange("p t c -> p c t"))
+
+        gather_x1(0)
+        gather_x1(1)
+        interleave_x1(0)
+        vs_plane = tile("vs_plane", [P, S], U8)
+        vs_gs = tile("vs_gs", [P, N], U8)
+        spread_scale_rows(vs_plane, vs_stage, 64)
+        nc.vector.tensor_copy(vs_gs[:], vs_plane[:].indirect(l6[:]))
+        gather_x1(2)
+        gather_x1(3)
+        for t in range(PACK):
+            nc.scalar.copy(b_t[t][:], b_ps[t][:])
+        gb = table.tile([P, PACK, O], F32, name="gb", align_bytes=64, offset=4 * T * 3)
+        for t in range(PACK):
+            nc.scalar.activation(gb[:, t, :], b_t[t][:].indirect(l5[:]), ACT.Copy, scale=sb_t[:, t : t + 1])
+
+        w_p = tile("w_p", [P, PACK, P], U16)
+        nc.vector.tensor_copy(w_p[:], w_raw[:].rearrange("p (m t) -> p t m", t=PACK))
+        interleave_x1(1)
+        x1_codes = [tile("x1_codes%d" % h, [P, P], U32) for h in range(2)]
+        x1_plane = [tile("x1_plane%d" % h, [P, P], U8) for h in range(2)]
+        for h in range(2):
+            nc.vector.quantize_mx(x1_codes[h][:].bitcast(E4M3), x1_plane[h][:], x1_il[h][:].rearrange("p c t -> p (c t)"))
+
+        a_ps = [psum.tile([P, J], F32, name="a_ps%d" % t) for t in range(PACK)]
+        a_t = [tile("a%d" % t, [P, J], F32) for t in range(PACK)]
+        for t in range(PACK):
+            for h in range(2):
+                nc.tensor.matmul_mx(a_ps[t][:, h * P : (h + 1) * P], lhsT=w_p[:, t, :].bitcast(E2M1),
+                                    lhsT_scale=w_plane[:, t, :], rhs=x1_codes[h][:].bitcast(E4M3),
+                                    rhs_scale=x1_plane[h][:], start=True, stop=True)
+
+        gate = [tile("gate%d" % u, [P, 2, O], F32) for u in range(2)]
+        ga = [tile("ga%d" % u, [P, 2, O], F32) for u in range(2)]
+        prod = [tile("prod%d" % u, [P, 2, O], F32) for u in range(2)]
+        hid_il = tile("hid_il", [P, O, PACK], BF16)
+        vs_gw = [tile("vs_gw%d" % h, [P, P], U32, tag=("x1_il1", "x1_codes0")[h]) for h in range(2)]
+
+        for t in range(PACK):
+            nc.vector.tensor_copy(a_t[t][:], a_ps[t][:])
+        for t in range(PACK):
+            u, e = divmod(t, 2)
+            nc.scalar.activation(gate[u][:, e, :], a_t[t][:].indirect(l4[:]), ACT.Sigmoid,
+                                 bias=b_t[t][:, 0:1], scale=sg_t[:, t : t + 1])
+            nc.scalar.activation(ga[u][:, e, :], a_t[t][:].indirect(l3[:]), ACT.Copy, scale=sa_t[:, t : t + 1])
+
+        def subtract_pair(u):
+            nc.vector.tensor_tensor(hid_il[:, :, 2 * u : 2 * u + 2], prod[u][:].rearrange("p t o -> p o t"),
+                                    gb[:, 2 * u : 2 * u + 2, :].rearrange("p t o -> p o t"), ALU.subtract)
+
+        nc.vector.tensor_tensor(prod[0][:], ga[0][:], gate[0][:], ALU.mult)
+        subtract_pair(0)
+        for e in range(2):
+            nc.vector.tensor_tensor(prod[1][:, e, :], ga[1][:, e, :], gate[1][:, e, :], ALU.mult)
+        subtract_pair(1)
+        hid_codes = tile("hid_codes", [P, O], U32)
+        hid_plane = tile("hid_plane", [P, O], U8)
+        nc.vector.quantize_mx(hid_codes[:].bitcast(E4M3), hid_plane[:], hid_il[:].rearrange("p o t -> p (o t)"))
+
+        for h in range(2):
+            nc.vector.tensor_copy(vs_gw[h][:], vs_w[:].indirect(l6[:, 8 * h : 8 * h + 8]))
+
+        p_ps = [psum.tile([P, O], F32, name="p_ps%d" % h, tag="bank_b%d" % h) for h in range(2)]
+        p_sb = [tile("p_sb%d" % h, [P, O], F32) for h in range(2)]
+        for h in range(2):
+            nc.tensor.matmul_mx(p_ps[h][:], lhsT=vs_gw[h][:].bitcast(E5M2), lhsT_scale=vs_gs[:, h * P : (h + 1) * P],
+                                rhs=hid_codes[:].bitcast(E4M3), rhs_scale=hid_plane[:], start=True, stop=True)
+        nc.scalar.copy(p_sb[0][:], p_ps[0][:])
+        nc.scalar.activation(pages[0][:].indirect(l7[:]), p_sb[0][:], ACT.Copy)
+        nc.scalar.dma_start(out[0:P, :], pages[0][:])
+        nc.vector.tensor_copy(p_sb[1][:], p_ps[1][:])
+        nc.vector.tensor_copy(pages[1][:].indirect(l7[:]), p_sb[1][:])
+        nc.sync.dma_start(out[P : 2 * P, :], pages[1][:])

@@ -71,6 +71,9 @@ def tile_list_offsetlead_codednote_store_scattered_kernel(
         sg_t = load_column_vector("sg_t", sg)
         sa_t = load_column_vector("sa_t", sa)
 
+        warm = tile("warm", [P, 8], F32)
+        nc.vector.memset(warm[:, 0:1], 0.0)
+        nc.scalar.activation(warm[:, 1:2], warm[:, 0:1], ACT.Sigmoid)
         xo_w = tile("xo_w", [P, Z], U16)
         w2_raw = tile("w2_raw", [P, R], U32)
         w_raw = tile("w_raw", [P, R], U16)

@@ -28,6 +28,7 @@ def tile_list_offsetlead_codednote_store_scattered_kernel(
     with ExitStack() as ctx:
         sb_pool = ctx.enter_context(tc.tile_pool(name="held", bufs=1))
         table = ctx.enter_context(tc.tile_pool(name="table", bufs=1))
+        shared = ctx.enter_context(tc.tile_pool(name="shared", bufs=1))
         psum = ctx.enter_context(tc.psum_pool(name="psum", bufs=1))
 
         def tile(name, shape, dtype, tag=None):
@@ -40,14 +41,13 @@ def tile_list_offsetlead_codednote_store_scattered_kernel(
 
         def load_column_vector(name, src):
             dst = tile(name, [P, PACK], F32)
-            nc.gpsimd.dma_start(dst[:], src.rearrange("(p t) o -> p (t o)", t=PACK))
+            nc.sync.dma_start(dst[:], src.rearrange("(p t) o -> p (t o)", t=PACK))
             return dst
 
-        def load_scale_rows(stage, first, scales):
+        def load_scale_rows(stage, first, scales, q):
             rows = scales[0].bitcast(I32).rearrange("(h q r) c -> q r h c", h=2, q=2)
-            for q in range(2):
-                part = first + 32 * q
-                nc.sync.dma_start(stage[part : part + 4].bitcast(I32), rows[q])
+            part = first + 32 * q
+            nc.sync.dma_start(stage[part : part + 4].bitcast(I32), rows[q])
 
         def spread_scale_rows(plane, stage, first):
             for h in range(2):
@@ -56,20 +56,15 @@ def tile_list_offsetlead_codednote_store_scattered_kernel(
 
         xo_stage = tile("xo_stage", [P, 2, Z], U8)
         w2_stage = tile("w2_stage", [P, 2, R], U8)
-        w_stage = tile("w_stage", [P, 2, R], U8)
-        vs_stage = tile("vs_stage", [P, 2, S], U8)
+        w_stage = shared.tile([P, 2, R], U8, name="w_stage", align_bytes=64, offset=512)
+        vs_rows = tile("vs_rows", [P, S], U8)
         pages = [tile("page%d" % h, [P, E], F32) for h in range(2)]
         nc.vector.memset(xo_stage[0:64].bitcast(I32), 0)
         nc.gpsimd.memset(w2_stage[64:128].bitcast(I32), 0)
-        nc.vector.memset(w_stage[0:64].bitcast(I32), 0)
-        nc.vector.memset(vs_stage[64:128].bitcast(I32), 0)
+        nc.vector.memset(w_stage[64:128].bitcast(I32), 0)
+        nc.vector.memset(vs_rows[:].bitcast(I32), 0)
         for page in pages:
             nc.vector.memset(page[:], 0.0)
-
-        gs_t = load_column_vector("gs_t", gs)
-        sb_t = load_column_vector("sb_t", sb)
-        sg_t = load_column_vector("sg_t", sg)
-        sa_t = load_column_vector("sa_t", sa)
 
         warm = tile("warm", [P, 8], F32)
         nc.vector.memset(warm[:, 0:1], 0.0)
@@ -82,23 +77,29 @@ def tile_list_offsetlead_codednote_store_scattered_kernel(
         cq_rows = cq.rearrange("(p t) c -> t p c", t=PACK)
 
         nc.sync.dma_start(xo_w[:].bitcast(I32), xo_words[0].bitcast(I32))
-        load_scale_rows(xo_stage, 0, xo_scales)
         l2 = load_list("l2", offs2)
+        for q in range(2):
+            load_scale_rows(xo_stage, 0, xo_scales, q)
+            load_scale_rows(w2_stage, 64, w2_scales, q)
         nc.sync.dma_start(w2_raw[:].bitcast(I32), w2_words[0].rearrange("p c r -> p (c r)").bitcast(I32))
-        load_scale_rows(w2_stage, 64, w2_scales)
         nc.sync.dma_start(cq_t[0][:], cq_rows[0])
         l1 = load_list("l1", offs)
-        load_scale_rows(w_stage, 0, w_scales)
+        gs_t = load_column_vector("gs_t", gs)
         nc.sync.dma_start(cq_t[1][:], cq_rows[1])
+        for q in range(2):
+            load_scale_rows(w_stage, 64, w_scales, q)
         nc.sync.dma_start(cq_t[2][:], cq_rows[2])
-        load_scale_rows(vs_stage, 64, vs_scales)
+        nc.sync.dma_start(vs_rows[0:P:8, :].bitcast(I32), vs_scales[0].bitcast(I32))
         l6 = load_list("l6", offs6)
         nc.sync.dma_start(cq_t[3][:], cq_rows[3])
         nc.sync.dma_start(w_raw[:].bitcast(I32), w_words[0].bitcast(I32))
         l5 = load_list("l5", offs5)
+        sb_t = load_column_vector("sb_t", sb)
         l4 = load_list("l4", offs4)
-        l3 = load_list("l3", offs3)
+        sg_t = load_column_vector("sg_t", sg)
         nc.sync.dma_start(vs_w[:].bitcast(I32), vs_words[0].rearrange("p c r -> p (c r)").bitcast(I32))
+        l3 = load_list("l3", offs3)
+        sa_t = load_column_vector("sa_t", sa)
         l7 = load_list("l7", offs7)
 
         xo_plane = tile("xo_plane", [P, Z], U8)
@@ -114,8 +115,8 @@ def tile_list_offsetlead_codednote_store_scattered_kernel(
         nc.vector.tensor_copy(w2_stage[0:64, 1, :].bitcast(I32), w2_stage[64:128, 0, :].bitcast(I32))
         nc.vector.tensor_copy(w2_plane[:], w2_stage[:, 1, :].rearrange("p (m t) -> p t m", t=PACK))
         w_plane = tile("w_plane", [P, PACK, P], U8)
-        nc.vector.tensor_copy(w_stage[64:128, 0, :].bitcast(I32), w_stage[0:64, 1, :].bitcast(I32))
-        nc.vector.tensor_copy(w_plane[:], w_stage[:, 0, :].rearrange("p (m t) -> p t m", t=PACK))
+        nc.vector.tensor_copy(w_stage[0:64, 1, :].bitcast(I32), w_stage[64:128, 0, :].bitcast(I32))
+        nc.vector.tensor_copy(w_plane[:], w_stage[:, 1, :].rearrange("p (m t) -> p t m", t=PACK))
 
         b_ps = [psum.tile([P, J], F32, name="b_ps%d" % t, tag="bank_b%d" % t) for t in range(PACK)]
         b_t = [table.tile([P, J], F32, name="b%d" % t, align_bytes=64, offset=4 * T * (1 + t // 2) + 4 * J * (t % 2))
@@ -125,7 +126,7 @@ def tile_list_offsetlead_codednote_store_scattered_kernel(
                                 rhs=xo_gw[:].bitcast(E2M1), rhs_scale=xo_gs[:], start=True, stop=True)
 
         x1_pair = [tile("x1_pair%d" % u, [P, 2, J], BF16) for u in range(2)]
-        x1_il = [tile("x1_il%d" % h, [P, P, PACK], BF16) for h in range(2)]
+        x1_il = [shared.tile([P, P, PACK], BF16, name="x1_il%d" % h, align_bytes=64, offset=1024 * h) for h in range(2)]
 
         def gather_x1(t):
             nc.scalar.activation(x1_pair[t // 2][:, t % 2, :], cq_t[t][:].indirect(l1[:]), ACT.Copy,
@@ -139,20 +140,25 @@ def tile_list_offsetlead_codednote_store_scattered_kernel(
         gather_x1(0)
         gather_x1(1)
         interleave_x1(0)
-        vs_plane = tile("vs_plane", [P, S], U8)
+        vs_picked = tile("vs_picked", [P, N], U8)
         vs_gs = tile("vs_gs", [P, N], U8)
-        spread_scale_rows(vs_plane, vs_stage, 64)
-        nc.vector.tensor_copy(vs_gs[:], vs_plane[:].indirect(l6[:]))
+        nc.vector.tensor_copy(vs_picked[:], vs_rows[:].indirect(l6[:]))
+        for r in range(4):
+            nc.sync.dma_start(vs_gs[r:P:32, :].bitcast(I32), vs_picked[8 * r : P : 32, :].bitcast(I32))
         gather_x1(2)
         gather_x1(3)
-        for t in range(PACK):
+        for t in range(2):
             nc.scalar.copy(b_t[t][:], b_ps[t][:])
+            nc.vector.tensor_copy(b_t[2 + t][:], b_ps[2 + t][:])
+        w_cols = w_raw[:].rearrange("p (m t) -> p t m", t=PACK)
+        w_p = [tile("w_p0", [P, 2, P], U16),
+               table.tile([P, 2, P], U16, name="w_p1", align_bytes=64, offset=4 * T * 3 + 4 * PACK * O)]
+        nc.scalar.copy(w_p[1][:], w_cols[:, 2:4, :])
         gb = table.tile([P, PACK, O], F32, name="gb", align_bytes=64, offset=4 * T * 3)
         for t in range(PACK):
             nc.scalar.activation(gb[:, t, :], b_t[t][:].indirect(l5[:]), ACT.Copy, scale=sb_t[:, t : t + 1])
 
-        w_p = tile("w_p", [P, PACK, P], U16)
-        nc.vector.tensor_copy(w_p[:], w_raw[:].rearrange("p (m t) -> p t m", t=PACK))
+        nc.vector.tensor_copy(w_p[0][:], w_cols[:, 0:2, :])
         interleave_x1(1)
         x1_codes = [tile("x1_codes%d" % h, [P, P], U32) for h in range(2)]
         x1_plane = [tile("x1_plane%d" % h, [P, P], U8) for h in range(2)]
@@ -163,7 +169,7 @@ def tile_list_offsetlead_codednote_store_scattered_kernel(
         a_t = [tile("a%d" % t, [P, J], F32) for t in range(PACK)]
         for t in range(PACK):
             for h in range(2):
-                nc.tensor.matmul_mx(a_ps[t][:, h * P : (h + 1) * P], lhsT=w_p[:, t, :].bitcast(E2M1),
+                nc.tensor.matmul_mx(a_ps[t][:, h * P : (h + 1) * P], lhsT=w_p[t // 2][:, t % 2, :].bitcast(E2M1),
                                     lhsT_scale=w_plane[:, t, :], rhs=x1_codes[h][:].bitcast(E4M3),
                                     rhs_scale=x1_plane[h][:], start=True, stop=True)
 
@@ -171,7 +177,8 @@ def tile_list_offsetlead_codednote_store_scattered_kernel(
         ga = [tile("ga%d" % u, [P, 2, O], F32) for u in range(2)]
         prod = [tile("prod%d" % u, [P, 2, O], F32) for u in range(2)]
         hid_il = tile("hid_il", [P, O, PACK], BF16)
-        vs_gw = [tile("vs_gw%d" % h, [P, P], U32, tag=("x1_il1", "x1_codes0")[h]) for h in range(2)]
+        vs_gw = [shared.tile([P, P], U32, name="vs_gw0", align_bytes=64, offset=1024),
+                 tile("vs_gw1", [P, P], U32, tag="x1_codes0")]
 
         for t in range(PACK):
             nc.vector.tensor_copy(a_t[t][:], a_ps[t][:])

@@ -97,9 +97,9 @@ def tile_list_offsetlead_codednote_store_scattered_kernel(
         sb_t = load_column_vector("sb_t", sb)
         l4 = load_list("l4", offs4)
         sg_t = load_column_vector("sg_t", sg)
-        nc.sync.dma_start(vs_w[:].bitcast(I32), vs_words[0].rearrange("p c r -> p (c r)").bitcast(I32))
         l3 = load_list("l3", offs3)
         sa_t = load_column_vector("sa_t", sa)
+        nc.sync.dma_start(vs_w[:].bitcast(I32), vs_words[0].rearrange("p c r -> p (c r)").bitcast(I32))
         l7 = load_list("l7", offs7)
 
         xo_plane = tile("xo_plane", [P, Z], U8)
@@ -160,54 +160,79 @@ def tile_list_offsetlead_codednote_store_scattered_kernel(
 
         nc.vector.tensor_copy(w_p[0][:], w_cols[:, 0:2, :])
         interleave_x1(1)
-        x1_codes = [tile("x1_codes%d" % h, [P, P], U32) for h in range(2)]
-        x1_plane = [tile("x1_plane%d" % h, [P, P], U8) for h in range(2)]
+        x1_codes = tile("x1_codes", [P, J], U32)
+        x1_plane = tile("x1_plane", [P, J], U8)
         for h in range(2):
-            nc.vector.quantize_mx(x1_codes[h][:].bitcast(E4M3), x1_plane[h][:], x1_il[h][:].rearrange("p c t -> p (c t)"))
+            cols = slice(h * P, (h + 1) * P)
+            nc.vector.quantize_mx(x1_codes[:, cols].bitcast(E4M3), x1_plane[:, cols],
+                                  x1_il[h][:].rearrange("p c t -> p (c t)"))
 
-        a_ps = [psum.tile([P, J], F32, name="a_ps%d" % t) for t in range(PACK)]
         a_t = [tile("a%d" % t, [P, J], F32) for t in range(PACK)]
-        for t in range(PACK):
-            for h in range(2):
-                nc.tensor.matmul_mx(a_ps[t][:, h * P : (h + 1) * P], lhsT=w_p[t // 2][:, t % 2, :].bitcast(E2M1),
-                                    lhsT_scale=w_plane[:, t, :], rhs=x1_codes[h][:].bitcast(E4M3),
-                                    rhs_scale=x1_plane[h][:], start=True, stop=True)
+        a0_ps = [psum.tile([P, P], F32, name="a0_ps0"), psum.tile([P, P], F32, name="a0_ps1", tag="bank_b3")]
+        a_ps = [psum.tile([P, J], F32, name="a_ps%d" % t) for t in range(1, PACK)]
 
-        gate = [tile("gate%d" % u, [P, 2, O], F32) for u in range(2)]
-        ga = [tile("ga%d" % u, [P, 2, O], F32) for u in range(2)]
-        prod = [tile("prod%d" % u, [P, 2, O], F32) for u in range(2)]
+        def product_a(acc, t, cols):
+            nc.tensor.matmul_mx(acc, lhsT=w_p[t // 2][:, t % 2, :].bitcast(E2M1), lhsT_scale=w_plane[:, t, :],
+                                rhs=x1_codes[:, cols].bitcast(E4M3), rhs_scale=x1_plane[:, cols], start=True, stop=True)
+
+        for h in range(2):
+            product_a(a0_ps[h][:], 0, slice(h * P, (h + 1) * P))
+        for t in range(1, PACK):
+            product_a(a_ps[t - 1][:], t, slice(0, J))
+        for h in range(2):
+            nc.vector.tensor_copy(a_t[0][:, h * P : (h + 1) * P], a0_ps[h][:])
+        for t in range(1, PACK):
+            nc.vector.tensor_copy(a_t[t][:], a_ps[t - 1][:])
+
+        HALF = O // 2
+        gate = [tile("gate%d" % t, [P, O], F32) for t in range(PACK)]
+        ga = [tile("ga%d" % t, [P, O], F32) for t in range(PACK)]
+        prod = [tile("prod%d" % u, [P, 2, 2, HALF], F32) for u in range(2)]
         hid_il = tile("hid_il", [P, O, PACK], BF16)
-        vs_gw = [shared.tile([P, P], U32, name="vs_gw0", align_bytes=64, offset=1024),
-                 tile("vs_gw1", [P, P], U32, tag="x1_codes0")]
-
-        for t in range(PACK):
-            nc.vector.tensor_copy(a_t[t][:], a_ps[t][:])
-        for t in range(PACK):
-            u, e = divmod(t, 2)
-            nc.scalar.activation(gate[u][:, e, :], a_t[t][:].indirect(l4[:]), ACT.Sigmoid,
-                                 bias=b_t[t][:, 0:1], scale=sg_t[:, t : t + 1])
-            nc.scalar.activation(ga[u][:, e, :], a_t[t][:].indirect(l3[:]), ACT.Copy, scale=sa_t[:, t : t + 1])
-
-        def subtract_pair(u):
-            nc.vector.tensor_tensor(hid_il[:, :, 2 * u : 2 * u + 2], prod[u][:].rearrange("p t o -> p o t"),
-                                    gb[:, 2 * u : 2 * u + 2, :].rearrange("p t o -> p o t"), ALU.subtract)
-
-        nc.vector.tensor_tensor(prod[0][:], ga[0][:], gate[0][:], ALU.mult)
-        subtract_pair(0)
-        for e in range(2):
-            nc.vector.tensor_tensor(prod[1][:, e, :], ga[1][:, e, :], gate[1][:, e, :], ALU.mult)
-        subtract_pair(1)
         hid_codes = tile("hid_codes", [P, O], U32)
         hid_plane = tile("hid_plane", [P, O], U8)
-        nc.vector.quantize_mx(hid_codes[:].bitcast(E4M3), hid_plane[:], hid_il[:].rearrange("p o t -> p (o t)"))
+        vs_gw = tile("vs_gw", [P, N], U32, tag="x1_codes")
+        nc.vector.tensor_copy(vs_gw[:], vs_w[:].indirect(l6[:]))
 
+        def gather_a(t, lo, hi):
+            nc.scalar.activation(gate[t][:, lo:hi], a_t[t][:].indirect(l4[:, lo // 16 : hi // 16]), ACT.Sigmoid,
+                                 bias=b_t[t][:, 0:1], scale=sg_t[:, t : t + 1])
+            nc.scalar.activation(ga[t][:, lo:hi], a_t[t][:].indirect(l3[:, lo // 16 : hi // 16]), ACT.Copy,
+                                 scale=sa_t[:, t : t + 1])
+
+        def multiply(t, halves):
+            cols = slice(halves.start * HALF, halves.stop * HALF)
+            nc.vector.tensor_tensor(prod[t // 2][:, halves, t % 2, :],
+                                    ga[t][:, cols].rearrange("p (h o) -> p h o", o=HALF),
+                                    gate[t][:, cols].rearrange("p (h o) -> p h o", o=HALF), ALU.mult)
+
+        def subtract_pair(u, halves):
+            cols = slice(halves.start * HALF, halves.stop * HALF)
+            nc.vector.tensor_tensor(hid_il[:, cols, 2 * u : 2 * u + 2].rearrange("p (h o) t -> p h o t", o=HALF),
+                                    prod[u][:, halves].rearrange("p h t o -> p h o t"),
+                                    gb[:, 2 * u : 2 * u + 2, cols].rearrange("p t (h o) -> p h o t", o=HALF),
+                                    ALU.subtract)
+
+        both = slice(0, 2)
+        for t in range(PACK - 1):
+            gather_a(t, 0, O)
+            multiply(t, both)
+            if t == 1:
+                subtract_pair(0, both)
         for h in range(2):
-            nc.vector.tensor_copy(vs_gw[h][:], vs_w[:].indirect(l6[:, 8 * h : 8 * h + 8]))
+            gather_a(PACK - 1, h * HALF, (h + 1) * HALF)
+            multiply(PACK - 1, slice(h, h + 1))
+        for h in range(2):
+            subtract_pair(1, slice(h, h + 1))
+        for lo in (0, HALF):
+            nc.vector.quantize_mx(hid_codes[:, lo : lo + HALF].bitcast(E4M3), hid_plane[:, lo : lo + HALF],
+                                  hid_il[:, lo : lo + HALF, :].rearrange("p o t -> p (o t)"))
+
 
         p_ps = [psum.tile([P, O], F32, name="p_ps%d" % h, tag="bank_b%d" % h) for h in range(2)]
         p_sb = [tile("p_sb%d" % h, [P, O], F32) for h in range(2)]
         for h in range(2):
-            nc.tensor.matmul_mx(p_ps[h][:], lhsT=vs_gw[h][:].bitcast(E5M2), lhsT_scale=vs_gs[:, h * P : (h + 1) * P],
+            nc.tensor.matmul_mx(p_ps[h][:], lhsT=vs_gw[:, h * P : (h + 1) * P].bitcast(E5M2), lhsT_scale=vs_gs[:, h * P : (h + 1) * P],
                                 rhs=hid_codes[:].bitcast(E4M3), rhs_scale=hid_plane[:], start=True, stop=True)
         nc.scalar.copy(p_sb[0][:], p_ps[0][:])
         nc.scalar.activation(pages[0][:].indirect(l7[:]), p_sb[0][:], ACT.Copy)

@@ -89,12 +89,12 @@ def tile_list_offsetlead_codednote_store_scattered_kernel(
         for q in range(2):
             load_scale_rows(w_stage, 64, w_scales, q)
         nc.sync.dma_start(cq_t[2][:], cq_rows[2])
-        nc.sync.dma_start(vs_rows[0:P:8, :].bitcast(I32), vs_scales[0].bitcast(I32))
-        l6 = load_list("l6", offs6)
         nc.sync.dma_start(cq_t[3][:], cq_rows[3])
         nc.sync.dma_start(w_raw[:].bitcast(I32), w_words[0].bitcast(I32))
         l5 = load_list("l5", offs5)
         sb_t = load_column_vector("sb_t", sb)
+        nc.sync.dma_start(vs_rows[0:P:8, :].bitcast(I32), vs_scales[0].bitcast(I32))
+        l6 = load_list("l6", offs6)
         l4 = load_list("l4", offs4)
         sg_t = load_column_vector("sg_t", sg)
         l3 = load_list("l3", offs3)
@@ -140,11 +140,6 @@ def tile_list_offsetlead_codednote_store_scattered_kernel(
         gather_x1(0)
         gather_x1(1)
         interleave_x1(0)
-        vs_picked = tile("vs_picked", [P, N], U8)
-        vs_gs = tile("vs_gs", [P, N], U8)
-        nc.vector.tensor_copy(vs_picked[:], vs_rows[:].indirect(l6[:]))
-        for r in range(4):
-            nc.sync.dma_start(vs_gs[r:P:32, :].bitcast(I32), vs_picked[8 * r : P : 32, :].bitcast(I32))
         gather_x1(2)
         gather_x1(3)
         for t in range(2):
@@ -166,6 +161,12 @@ def tile_list_offsetlead_codednote_store_scattered_kernel(
             cols = slice(h * P, (h + 1) * P)
             nc.vector.quantize_mx(x1_codes[:, cols].bitcast(E4M3), x1_plane[:, cols],
                                   x1_il[h][:].rearrange("p c t -> p (c t)"))
+
+        vs_picked = shared.tile([P, N], U8, name="vs_picked", align_bytes=64, offset=1024)
+        vs_gs = tile("vs_gs", [P, N], U8)
+        nc.vector.tensor_copy(vs_picked[:], vs_rows[:].indirect(l6[:]))
+        for r in range(4):
+            nc.sync.dma_start(vs_gs[r:P:32, :].bitcast(I32), vs_picked[8 * r : P : 32, :].bitcast(I32))
 
         a_t = [tile("a%d" % t, [P, J], F32) for t in range(PACK)]
         a0_ps = [psum.tile([P, P], F32, name="a0_ps0"), psum.tile([P, P], F32, name="a0_ps1", tag="bank_b3")]

from contextlib import ExitStack

import concourse.mybir as mybir

K, T, J, R, F, Z, O, N, S, E = 512, 1024, 256, 512, 512, 1024, 128, 256, 1024, 1024
FLOPS = 2 * K * R * J + 2 * F * R * J + 2 * R * N * O

P = 128
PACK = 4
F32 = mybir.dt.float32
BF16 = mybir.dt.bfloat16
I32 = mybir.dt.int32
U32 = mybir.dt.uint32
U16 = mybir.dt.uint16
U8 = mybir.dt.uint8
E4M3 = mybir.dt.float8_e4m3fn_x4
E5M2 = mybir.dt.float8_e5m2_x4
E2M1 = mybir.dt.float4_e2m1fn_x4
ACT = mybir.ActivationFunctionType
ALU = mybir.AluOpType


def tile_list_offsetlead_codednote_store_scattered_kernel(
    tc, xo_words, xo_scales, cq, gs, w_words, w_scales, w2_words, w2_scales, sa, sb, sg,
    vs_words, vs_scales, offs, offs2, offs3, offs4, offs5, offs6, offs7, out,
):
    nc = tc.nc
    with ExitStack() as ctx:
        sb_pool = ctx.enter_context(tc.tile_pool(name="held", bufs=1))
        table = ctx.enter_context(tc.tile_pool(name="table", bufs=1))
        shared = ctx.enter_context(tc.tile_pool(name="shared", bufs=1))
        psum = ctx.enter_context(tc.psum_pool(name="psum", bufs=1))

        def tile(name, shape, dtype, tag=None):
            return sb_pool.tile(shape, dtype, name=name, tag=tag or name, align_bytes=64)

        def load_list(name, src):
            dst = sb_pool.tile(list(src.shape), U16, name=name)
            nc.sync.dma_start(dst[:], src)
            return dst

        def load_column_vector(name, src):
            dst = tile(name, [P, PACK], F32)
            nc.sync.dma_start(dst[:], src.rearrange("(p t) o -> p (t o)", t=PACK))
            return dst

        def load_scale_rows(stage, first, scales, q):
            rows = scales[0].bitcast(I32).rearrange("(h q r) c -> q r h c", h=2, q=2)
            part = first + 32 * q
            nc.sync.dma_start(stage[part : part + 4].bitcast(I32), rows[q])

        def spread_scale_rows(plane, stage, first):
            for h in range(2):
                nc.vector.tensor_copy(plane[64 * h : 64 * h + 64, :].bitcast(I32),
                                      stage[first : first + 64, h, :].bitcast(I32))

        xo_stage = tile("xo_stage", [P, 2, Z], U8)
        w2_stage = tile("w2_stage", [P, 2, R], U8)
        w_stage = shared.tile([P, 2, R], U8, name="w_stage", align_bytes=64, offset=512)
        vs_rows = tile("vs_rows", [P, S], U8)
        pages = [tile("page%d" % h, [P, E], F32) for h in range(2)]
        nc.vector.memset(xo_stage[0:64].bitcast(I32), 0)
        nc.gpsimd.memset(w2_stage[64:128].bitcast(I32), 0)
        nc.vector.memset(w_stage[64:128].bitcast(I32), 0)
        nc.vector.memset(vs_rows[:].bitcast(I32), 0)
        for page in pages:
            nc.vector.memset(page[:], 0.0)

        warm = tile("warm", [P, 8], F32)
        nc.vector.memset(warm[:, 0:1], 0.0)
        nc.scalar.activation(warm[:, 1:2], warm[:, 0:1], ACT.Sigmoid)
        xo_w = tile("xo_w", [P, Z], U16)
        w2_raw = tile("w2_raw", [P, R], U32)
        w_raw = tile("w_raw", [P, R], U16)
        vs_w = tile("vs_w", [P, S], U32)
        cq_t = [table.tile([P, T], F32, name="cq%d" % t, align_bytes=64, offset=4 * T * t) for t in range(PACK)]
        cq_rows = cq.rearrange("(p t) c -> t p c", t=PACK)

        nc.sync.dma_start(xo_w[:].bitcast(I32), xo_words[0].bitcast(I32))
        l2 = load_list("l2", offs2)
        for q in range(2):
            load_scale_rows(xo_stage, 0, xo_scales, q)
            load_scale_rows(w2_stage, 64, w2_scales, q)
        nc.sync.dma_start(w2_raw[:].bitcast(I32), w2_words[0].rearrange("p c r -> p (c r)").bitcast(I32))
        nc.sync.dma_start(cq_t[0][:], cq_rows[0])
        l1 = load_list("l1", offs)
        gs_t = load_column_vector("gs_t", gs)
        nc.sync.dma_start(cq_t[1][:], cq_rows[1])
        for q in range(2):
            load_scale_rows(w_stage, 64, w_scales, q)
        nc.sync.dma_start(cq_t[2][:], cq_rows[2])
        nc.sync.dma_start(cq_t[3][:], cq_rows[3])
        nc.sync.dma_start(w_raw[:].bitcast(I32), w_words[0].bitcast(I32))
        l5 = load_list("l5", offs5)
        sb_t = load_column_vector("sb_t", sb)
        nc.sync.dma_start(vs_rows[0:P:8, :].bitcast(I32), vs_scales[0].bitcast(I32))
        l6 = load_list("l6", offs6)
        l4 = load_list("l4", offs4)
        sg_t = load_column_vector("sg_t", sg)
        l3 = load_list("l3", offs3)
        sa_t = load_column_vector("sa_t", sa)
        nc.sync.dma_start(vs_w[:].bitcast(I32), vs_words[0].rearrange("p c r -> p (c r)").bitcast(I32))
        l7 = load_list("l7", offs7)

        xo_plane = tile("xo_plane", [P, Z], U8)
        xo_gw = tile("xo_gw", [P, J], U16)
        xo_gs = tile("xo_gs", [P, J], U8)
        nc.vector.tensor_copy(xo_gw[:], xo_w[:].indirect(l2[:]))
        spread_scale_rows(xo_plane, xo_stage, 0)
        nc.vector.tensor_copy(xo_gs[:], xo_plane[:].indirect(l2[:]))

        w2_p = tile("w2_p", [P, PACK, P], U32)
        nc.scalar.copy(w2_p[:].rearrange("p t m -> p m t"), w2_raw[:].rearrange("p (m t) -> p m t", t=PACK))
        w2_plane = tile("w2_plane", [P, PACK, P], U8)
        nc.vector.tensor_copy(w2_stage[0:64, 1, :].bitcast(I32), w2_stage[64:128, 0, :].bitcast(I32))
        nc.vector.tensor_copy(w2_plane[:], w2_stage[:, 1, :].rearrange("p (m t) -> p t m", t=PACK))
        w_plane = tile("w_plane", [P, PACK, P], U8)
        nc.vector.tensor_copy(w_stage[0:64, 1, :].bitcast(I32), w_stage[64:128, 0, :].bitcast(I32))
        nc.vector.tensor_copy(w_plane[:], w_stage[:, 1, :].rearrange("p (m t) -> p t m", t=PACK))

        b_ps = [psum.tile([P, J], F32, name="b_ps%d" % t, tag="bank_b%d" % t) for t in range(PACK)]
        b_t = [table.tile([P, J], F32, name="b%d" % t, align_bytes=64, offset=4 * T * (1 + t // 2) + 4 * J * (t % 2))
               for t in range(PACK)]
        for t in range(PACK):
            nc.tensor.matmul_mx(b_ps[t][:], lhsT=w2_p[:, t, :].bitcast(E5M2), lhsT_scale=w2_plane[:, t, :],
                                rhs=xo_gw[:].bitcast(E2M1), rhs_scale=xo_gs[:], start=True, stop=True)

        x1_pair = [tile("x1_pair%d" % u, [P, 2, J], BF16) for u in range(2)]
        x1_il = [shared.tile([P, P, PACK], BF16, name="x1_il%d" % h, align_bytes=64, offset=1024 * h) for h in range(2)]

        def gather_x1(t):
            nc.scalar.activation(x1_pair[t // 2][:, t % 2, :], cq_t[t][:].indirect(l1[:]), ACT.Copy,
                                 scale=gs_t[:, t : t + 1])

        def interleave_x1(u):
            for h in range(2):
                nc.vector.tensor_copy(x1_il[h][:, :, 2 * u : 2 * u + 2],
                                      x1_pair[u][:, :, h * P : (h + 1) * P].rearrange("p t c -> p c t"))

        gather_x1(0)
        gather_x1(1)
        interleave_x1(0)
        gather_x1(2)
        gather_x1(3)
        for t in range(2):
            nc.scalar.copy(b_t[t][:], b_ps[t][:])
            nc.vector.tensor_copy(b_t[2 + t][:], b_ps[2 + t][:])
        w_cols = w_raw[:].rearrange("p (m t) -> p t m", t=PACK)
        w_p = [tile("w_p0", [P, 2, P], U16),
               table.tile([P, 2, P], U16, name="w_p1", align_bytes=64, offset=4 * T * 3 + 4 * PACK * O)]
        nc.scalar.copy(w_p[1][:], w_cols[:, 2:4, :])
        gb = table.tile([P, PACK, O], F32, name="gb", align_bytes=64, offset=4 * T * 3)
        for t in range(PACK):
            nc.scalar.activation(gb[:, t, :], b_t[t][:].indirect(l5[:]), ACT.Copy, scale=sb_t[:, t : t + 1])

        nc.vector.tensor_copy(w_p[0][:], w_cols[:, 0:2, :])
        interleave_x1(1)
        x1_codes = tile("x1_codes", [P, J], U32)
        x1_plane = tile("x1_plane", [P, J], U8)
        for h in range(2):
            cols = slice(h * P, (h + 1) * P)
            nc.vector.quantize_mx(x1_codes[:, cols].bitcast(E4M3), x1_plane[:, cols],
                                  x1_il[h][:].rearrange("p c t -> p (c t)"))

        vs_picked = shared.tile([P, N], U8, name="vs_picked", align_bytes=64, offset=1024)
        vs_gs = tile("vs_gs", [P, N], U8)
        nc.vector.tensor_copy(vs_picked[:], vs_rows[:].indirect(l6[:]))
        for r in range(4):
            nc.sync.dma_start(vs_gs[r:P:32, :].bitcast(I32), vs_picked[8 * r : P : 32, :].bitcast(I32))

        a_t = [tile("a%d" % t, [P, J], F32) for t in range(PACK)]
        a0_ps = [psum.tile([P, P], F32, name="a0_ps0"), psum.tile([P, P], F32, name="a0_ps1", tag="bank_b3")]
        a_ps = [psum.tile([P, J], F32, name="a_ps%d" % t) for t in range(1, PACK)]

        def product_a(acc, t, cols):
            nc.tensor.matmul_mx(acc, lhsT=w_p[t // 2][:, t % 2, :].bitcast(E2M1), lhsT_scale=w_plane[:, t, :],
                                rhs=x1_codes[:, cols].bitcast(E4M3), rhs_scale=x1_plane[:, cols], start=True, stop=True)

        for h in range(2):
            product_a(a0_ps[h][:], 0, slice(h * P, (h + 1) * P))
        for t in range(1, PACK):
            product_a(a_ps[t - 1][:], t, slice(0, J))
        for h in range(2):
            nc.vector.tensor_copy(a_t[0][:, h * P : (h + 1) * P], a0_ps[h][:])
        for t in range(1, PACK):
            nc.vector.tensor_copy(a_t[t][:], a_ps[t - 1][:])

        HALF = O // 2
        gate = [tile("gate%d" % t, [P, O], F32) for t in range(PACK)]
        ga = [tile("ga%d" % t, [P, O], F32) for t in range(PACK)]
        prod = [tile("prod%d" % u, [P, 2, 2, HALF], F32) for u in range(2)]
        hid_il = tile("hid_il", [P, O, PACK], BF16)
        hid_codes = tile("hid_codes", [P, O], U32)
        hid_plane = tile("hid_plane", [P, O], U8)
        vs_gw = tile("vs_gw", [P, N], U32, tag="x1_codes")
        nc.vector.tensor_copy(vs_gw[:], vs_w[:].indirect(l6[:]))

        def gather_a(t, lo, hi):
            nc.scalar.activation(gate[t][:, lo:hi], a_t[t][:].indirect(l4[:, lo // 16 : hi // 16]), ACT.Sigmoid,
                                 bias=b_t[t][:, 0:1], scale=sg_t[:, t : t + 1])
            nc.scalar.activation(ga[t][:, lo:hi], a_t[t][:].indirect(l3[:, lo // 16 : hi // 16]), ACT.Copy,
                                 scale=sa_t[:, t : t + 1])

        def multiply(t, halves):
            cols = slice(halves.start * HALF, halves.stop * HALF)
            nc.vector.tensor_tensor(prod[t // 2][:, halves, t % 2, :],
                                    ga[t][:, cols].rearrange("p (h o) -> p h o", o=HALF),
                                    gate[t][:, cols].rearrange("p (h o) -> p h o", o=HALF), ALU.mult)

        def subtract_pair(u, halves):
            cols = slice(halves.start * HALF, halves.stop * HALF)
            nc.vector.tensor_tensor(hid_il[:, cols, 2 * u : 2 * u + 2].rearrange("p (h o) t -> p h o t", o=HALF),
                                    prod[u][:, halves].rearrange("p h t o -> p h o t"),
                                    gb[:, 2 * u : 2 * u + 2, cols].rearrange("p t (h o) -> p h o t", o=HALF),
                                    ALU.subtract)

        both = slice(0, 2)
        for t in range(PACK - 1):
            gather_a(t, 0, O)
            multiply(t, both)
            if t == 1:
                subtract_pair(0, both)
        for h in range(2):
            gather_a(PACK - 1, h * HALF, (h + 1) * HALF)
            multiply(PACK - 1, slice(h, h + 1))
        for h in range(2):
            subtract_pair(1, slice(h, h + 1))
        for lo in (0, HALF):
            nc.vector.quantize_mx(hid_codes[:, lo : lo + HALF].bitcast(E4M3), hid_plane[:, lo : lo + HALF],
                                  hid_il[:, lo : lo + HALF, :].rearrange("p o t -> p (o t)"))


        p_ps = [psum.tile([P, O], F32, name="p_ps%d" % h, tag="bank_b%d" % h) for h in range(2)]
        p_sb = [tile("p_sb%d" % h, [P, O], F32) for h in range(2)]
        for h in range(2):
            nc.tensor.matmul_mx(p_ps[h][:], lhsT=vs_gw[:, h * P : (h + 1) * P].bitcast(E5M2), lhsT_scale=vs_gs[:, h * P : (h + 1) * P],
                                rhs=hid_codes[:].bitcast(E4M3), rhs_scale=hid_plane[:], start=True, stop=True)
        nc.scalar.copy(p_sb[0][:], p_ps[0][:])
        nc.scalar.activation(pages[0][:].indirect(l7[:]), p_sb[0][:], ACT.Copy)
        nc.scalar.dma_start(out[0:P, :], pages[0][:])
        nc.vector.tensor_copy(p_sb[1][:], p_ps[1][:])
        nc.vector.tensor_copy(pages[1][:].indirect(l7[:]), p_sb[1][:])
        nc.sync.dma_start(out[P : 2 * P, :], pages[1][:])
